import numpy as np
import ml_dtypes


def mxq(x, axis, fmt="e4m3"):
    dtype, down = {"e4m3": (ml_dtypes.float8_e4m3fn, 7), "e5m2": (ml_dtypes.float8_e5m2, 14)}[fmt]
    v = np.moveaxis(np.asarray(x, np.float32).astype(ml_dtypes.bfloat16).astype(np.float64), axis, -1)
    blocks = v.reshape(v.shape[:-1] + (-1, 32))
    amax = np.abs(blocks).max(-1, keepdims=True)
    byte = np.maximum(np.where(amax > 0, np.frexp(amax)[1] - 1 + 127, 0) - down, 1)
    scale = np.exp2(byte - 127.0)
    codes = (blocks / scale).astype(np.float32).astype(dtype).astype(np.float64)
    return np.moveaxis((codes * scale).reshape(v.shape), -1, axis)


WIDE = False


def mx_kscale(k):
    if not WIDE:
        return np.ones(k)
    levels = np.array([10, -10, 5, -5, 0])
    if k % 512:
        return np.exp2(np.random.permutation(np.resize(levels, k // 32))).repeat(32)
    a = np.empty((k // 512, 16))
    for p in range(k // 512):
        a[p, :8] = np.random.permutation(np.resize(levels, 8))
        for g in range(8):
            far = levels[np.abs(levels - a[p, g]) >= 10]
            a[p, g + 8] = far[np.random.randint(len(far))]
    return np.exp2(a.ravel()).repeat(32)


def f64(x):
    return np.asarray(x).astype(np.float64)


def striped(idx):
    return np.tile(idx.reshape(-1, 16).T, (8, 1)).astype(np.uint16)


def unstriped(offs):
    return offs[:16].T.reshape(-1).astype(np.int64)


def pack_weight(w):
    k, n = w.shape
    w = f64(np.asarray(w, np.float32).astype(ml_dtypes.bfloat16)).reshape(k // 32, 32, n)
    amax = np.abs(w).max(1)
    byte = np.clip(np.where(amax > 0, np.frexp(amax)[1] - 1 + 127 - 7, 1), 1, 254)
    scaled = (w * np.exp2(127.0 - byte)[:, None, :]).reshape(k, n).astype(np.float32)
    words = np.ascontiguousarray(scaled.reshape(k // 512, 128, 4, n).transpose(0, 1, 3, 2)).astype(ml_dtypes.float8_e4m3fn).view(np.uint8)
    return words, np.ascontiguousarray(byte.astype(np.uint8).reshape(k // 512, 16, n))


def unpack_weight(words, scales):
    g, p, n, _ = words.shape
    vals = np.ascontiguousarray(words).view(ml_dtypes.float8_e4m3fn).astype(np.float64) * np.repeat(np.exp2(scales.astype(np.float64) - 127.0), 8, axis=1)[..., None]
    return vals.transpose(0, 1, 3, 2).reshape(g * 512, n)


K, T, S, V, R = 1024, 2048, 512, 256, 128


def setup_inputs():
    n = np.random.standard_normal
    s = mx_kscale(K)[:, None]
    c = mx_kscale(S)
    packed_xT = pack_weight(n((K, T)) * s)
    return {
        "x_words": packed_xT[0],
        "x_scales": packed_xT[1],
        "qT": (n((K, V)) / np.sqrt(K) / s).astype(np.float32),
        "term": (np.random.uniform(0.0, 2.0, (S, R)) / S / c[:, None]).astype(np.float32),
        "prior": (0.4 * n((S, 1))).astype(np.float32),
        "lenw": (np.random.uniform(0.5, 1.5, (S, 1)) * c[:, None]).astype(np.float32),
        "orig": (np.random.uniform(0.0, 2.0, (R, V))).astype(np.float32),
        "offs": striped(np.random.permutation(T)[:S]),
    }


def reference(x_words, x_scales, qT, term, prior, lenw, orig, offs):
    xq = unpack_weight(x_words, x_scales)[:, unstriped(offs)]
    qTq = mxq(f64(qT), 0, "e4m3")
    y = xq.T @ qTq
    pd = np.exp(0.8 * y + f64(prior))
    wd = f64(lenw) * pd
    fb = mxq(f64(term), 0, "e4m3").T @ mxq(wd, 0, "e4m3")
    return 0.5 * fb + 0.5 * f64(orig)

@@ -1,0 +1,181 @@
+from contextlib import ExitStack
+
+import concourse.mybir as mybir
+
+K, T, S, V, R = 1024, 2048, 512, 256, 128
+FLOPS = 2 * K * S * V + 2 * S * R * V
+
+F32 = mybir.dt.float32
+BF16 = mybir.dt.bfloat16
+I32 = mybir.dt.int32
+U32 = mybir.dt.uint32
+U16 = mybir.dt.uint16
+U8 = mybir.dt.uint8
+FP8X4 = mybir.dt.float8_e4m3fn_x4
+ACT = mybir.ActivationFunctionType
+ALU = mybir.AluOpType
+
+P = 128
+PACK = 4
+PASSES = K // (P * PACK)
+HALF = V // 2
+RUN = 4
+
+
+def interleave(copy, grouped, raw):
+    copy(
+        out=grouped.rearrange("p (c i) j -> p c j i", i=RUN),
+        in_=raw.rearrange("p j (c i) -> p c j i", i=RUN),
+    )
+
+
+def tile_picked_yrm3_mix_p_kernel(
+    tc, x_words, x_scales, qT, term, prior, lenw, orig, offs, out
+):
+    nc = tc.nc
+    with ExitStack() as ctx:
+        keep = ctx.enter_context(tc.tile_pool(name="keep", bufs=1))
+        psum = ctx.enter_context(tc.psum_pool(name="psum", bufs=8))
+
+        def quantize(grouped, width, name):
+            codes = keep.tile([P, width], U32, name=name + "_codes", align_bytes=64)
+            scales = keep.tile([P, width], U8, name=name + "_scales", align_bytes=64)
+            nc.vector.quantize_mx(
+                out=codes[:].bitcast(FP8X4),
+                scales=scales[:],
+                in_=grouped[:].rearrange("p w j -> p (w j)"),
+            )
+            return codes, scales
+
+        scale_table = keep.tile([P, T], U8, name="scale_table", align_bytes=64)
+        nc.vector.memset(scale_table[:].bitcast(I32), 0)
+        scale_queues = [nc.scalar, nc.scalar, nc.scalar, nc.scalar]
+        for quad in range(4):
+            scale_queues[quad].dma_start(
+                out=scale_table[32 * quad : 32 * quad + 4 * PASSES, :].bitcast(I32),
+                in_=x_scales[:, 4 * quad : 4 * quad + 4, :].bitcast(I32),
+            )
+
+        def scalar_cast(out, in_):
+            nc.scalar.activation(out=out, in_=in_, func=ACT.Copy)
+
+        prior_sb = keep.tile([P, PACK], F32, name="prior_sb")
+        lenw_sb = keep.tile([P, PACK], F32, name="lenw_sb")
+        nc.gpsimd.dma_start(out=prior_sb[:], in_=prior.rearrange("(p j) o -> p (j o)", j=PACK))
+        nc.gpsimd.dma_start(out=lenw_sb[:], in_=lenw.rearrange("(p j) o -> p (j o)", j=PACK))
+
+        offsets = keep.tile([P, S // 16], U16, name="offsets")
+        nc.sync.dma_start(offsets[:], offs)
+
+        word_table = [keep.tile([P, T], U32, name="word_table%d" % g, align_bytes=64) for g in range(PASSES)]
+
+        def load_words(g):
+            nc.sync.dma_start(
+                out=word_table[g][:].bitcast(I32),
+                in_=x_words[g].rearrange("p n t -> p (n t)").bitcast(I32),
+            )
+
+        q_rows = qT.rearrange("(g p j) v -> g p j v", g=PASSES, j=PACK)
+        q0_raw = keep.tile([P, PACK, V], F32, name="q0_raw", tag="stage_a")
+        q1a_raw = keep.tile([P, PACK, HALF], F32, name="q1a_raw", tag="stage_b")
+        load_words(0)
+        nc.sync.dma_start(out=q0_raw[:], in_=q_rows[0])
+        nc.sync.dma_start(out=q1a_raw[:], in_=q_rows[1][:, :, 0:HALF])
+        load_words(1)
+
+        def gather_words(g):
+            picked = keep.tile([P, S], U32, name="picked_words%d" % g, align_bytes=64)
+            nc.vector.tensor_copy(
+                out=picked[:].rearrange("p (j m) -> p m j", j=PACK),
+                in_=word_table[g][:].indirect(offsets[:]),
+            )
+            return picked
+
+        picked_words = [gather_words(0)]
+        listed_scales = keep.tile([P, S], U8, name="listed_scales", align_bytes=64)
+        picked_scales = keep.tile([P, S], U8, name="picked_scales", align_bytes=64)
+        nc.vector.tensor_copy(out=listed_scales[:], in_=scale_table[:].indirect(offsets[:]))
+        nc.vector.tensor_copy(
+            out=picked_scales[:].rearrange("p (j m) -> p j m", j=PACK),
+            in_=listed_scales[:].rearrange("p (m j) -> p j m", j=PACK),
+        )
+
+        q0_bf = keep.tile([P, V, PACK], BF16, name="q0_bf", align_bytes=64)
+        q1a_bf = keep.tile([P, HALF, PACK], BF16, name="q1a_bf", tag="stage_c", align_bytes=64)
+        q1b_bf = keep.tile([P, HALF, PACK], BF16, name="q1b_bf", align_bytes=64)
+        interleave(scalar_cast, q0_bf[:], q0_raw[:])
+        interleave(scalar_cast, q1a_bf[:], q1a_raw[:])
+        q0_codes, q0_scales = quantize(q0_bf, V, "q0")
+        q1a = quantize(q1a_bf, HALF, "q1a")
+
+        q1b_raw = keep.tile([P, PACK, HALF], F32, name="q1b_raw", tag="stage_a")
+        term_raw = keep.tile([P, PACK, R], F32, name="term_raw", tag="stage_b")
+        orig_sb = keep.tile([P, V], F32, name="orig_sb", tag="stage_c", align_bytes=64)
+        nc.sync.dma_start(out=q1b_raw[:], in_=q_rows[1][:, :, HALF:V])
+        nc.sync.dma_start(out=term_raw[:], in_=term.rearrange("(p j) r -> p j r", j=PACK))
+        nc.sync.dma_start(out=orig_sb[:], in_=orig)
+
+        def score_pass(bank, g, j, codes, scales):
+            cols = slice(j * P, (j + 1) * P)
+            nc.tensor.matmul_mx(
+                out=bank[:],
+                lhsT=picked_words[g][:, cols].bitcast(FP8X4),
+                lhsT_scale=picked_scales[4 * g :, cols],
+                rhs=codes.bitcast(FP8X4),
+                rhs_scale=scales,
+                start=(g == 0),
+                stop=(g == PASSES - 1),
+            )
+
+        banks = [[psum.tile([P, HALF], F32, name="bank%d%d" % (h, j), tag="bank") for j in range(PACK)] for h in range(2)]
+        for h in range(2):
+            cols = slice(h * HALF, (h + 1) * HALF)
+            for j in range(PACK):
+                score_pass(banks[h][j], 0, j, q0_codes[:, cols], q0_scales[:, cols])
+
+        picked_words.append(gather_words(1))
+        interleave(scalar_cast, q1b_bf[:], q1b_raw[:])
+        q1b = quantize(q1b_bf, HALF, "q1b")
+        term_bf = keep.tile([P, R, PACK], BF16, name="term_bf", align_bytes=64)
+        interleave(nc.vector.tensor_copy, term_bf[:], term_raw[:])
+        term_codes, term_scales = quantize(term_bf, R, "term")
+
+        pd = []
+        for h, (codes, scales) in enumerate([q1a, q1b]):
+            pd_h = keep.tile([P, PACK, HALF], F32, name="pd%d" % h)
+            for j in range(PACK):
+                score_pass(banks[h][j], 1, j, codes[:], scales[:])
+                nc.scalar.activation(
+                    out=pd_h[:, j, :], in_=banks[h][j][:], func=ACT.Exp, bias=prior_sb[:, j : j + 1], scale=0.8
+                )
+            pd.append(pd_h)
+
+        half_orig = keep.tile([P, V], F32, name="half_orig")
+        nc.scalar.mul(out=half_orig[:], in_=orig_sb[:], mul=0.5)
+
+        lenw_wide = lenw_sb[:].unsqueeze(1).unsqueeze(3).to_broadcast([P, HALF // RUN, PACK, RUN])
+        for h in range(2):
+            cols = slice(h * HALF, (h + 1) * HALF)
+            wd_bf = keep.tile([P, HALF, PACK], BF16, name="wd_bf%d" % h, align_bytes=64)
+            nc.vector.tensor_tensor(
+                out=wd_bf[:].rearrange("p (c i) j -> p c j i", i=RUN),
+                in0=pd[h][:].rearrange("p j (c i) -> p c j i", i=RUN),
+                in1=lenw_wide,
+                op=ALU.mult,
+            )
+            wd_codes, wd_scales = quantize(wd_bf, HALF, "wd%d" % h)
+            fb = psum.tile([P, HALF], F32, name="fb%d" % h, tag="bank")
+            nc.tensor.matmul_mx(
+                out=fb[:],
+                lhsT=term_codes[:].bitcast(FP8X4),
+                lhsT_scale=term_scales[:],
+                rhs=wd_codes[:].bitcast(FP8X4),
+                rhs_scale=wd_scales[:],
+                start=True,
+                stop=True,
+            )
+            mixed = keep.tile([P, HALF], F32, name="mixed%d" % h)
+            nc.vector.scalar_tensor_tensor(
+                out=mixed[:], in0=fb[:], scalar=0.5, in1=half_orig[:, cols], op0=ALU.mult, op1=ALU.add
+            )
+            nc.sync.dma_start(out=out[:, cols], in_=mixed[:])

@@ -35,10 +35,10 @@ def tile_picked_yrm3_mix_p_kernel(
     nc = tc.nc
     with ExitStack() as ctx:
         keep = ctx.enter_context(tc.tile_pool(name="keep", bufs=1))
-        psum = ctx.enter_context(tc.psum_pool(name="psum", bufs=8))
+        psum = ctx.enter_context(tc.psum_pool(name="psum", bufs=1))
 
-        def quantize(grouped, width, name):
-            codes = keep.tile([P, width], U32, name=name + "_codes", align_bytes=64)
+        def quantize(grouped, width, name, tag=None):
+            codes = keep.tile([P, width], U32, name=name + "_codes", tag=tag or name + "_codes", align_bytes=64)
             scales = keep.tile([P, width], U8, name=name + "_scales", align_bytes=64)
             nc.vector.quantize_mx(
                 out=codes[:].bitcast(FP8X4),
@@ -56,6 +56,9 @@ def tile_picked_yrm3_mix_p_kernel(
                 in_=x_scales[:, 4 * quad : 4 * quad + 4, :].bitcast(I32),
             )
 
+        def vector_half(out, in_):
+            nc.vector.tensor_scalar(out=out, in0=in_, scalar1=0.5, scalar2=None, op0=ALU.mult)
+
         def scalar_cast(out, in_):
             nc.scalar.activation(out=out, in_=in_, func=ACT.Copy)
 
@@ -67,7 +70,7 @@ def tile_picked_yrm3_mix_p_kernel(
         offsets = keep.tile([P, S // 16], U16, name="offsets")
         nc.sync.dma_start(offsets[:], offs)
 
-        word_table = [keep.tile([P, T], U32, name="word_table%d" % g, align_bytes=64) for g in range(PASSES)]
+        word_table = [keep.tile([P, T], U32, name="word_table%d" % g, tag="word_table%d" % g, align_bytes=64) for g in range(PASSES)]
 
         def load_words(g):
             nc.sync.dma_start(
@@ -77,7 +80,7 @@ def tile_picked_yrm3_mix_p_kernel(
 
         q_rows = qT.rearrange("(g p j) v -> g p j v", g=PASSES, j=PACK)
         q0_raw = keep.tile([P, PACK, V], F32, name="q0_raw", tag="stage_a")
-        q1a_raw = keep.tile([P, PACK, HALF], F32, name="q1a_raw", tag="stage_b")
+        q1a_raw = keep.tile([P, PACK, HALF], F32, name="q1a_raw", tag="stage_b", align_bytes=64)
         load_words(0)
         nc.sync.dma_start(out=q0_raw[:], in_=q_rows[0])
         nc.sync.dma_start(out=q1a_raw[:], in_=q_rows[1][:, :, 0:HALF])
@@ -102,14 +105,14 @@ def tile_picked_yrm3_mix_p_kernel(
 
         q0_bf = keep.tile([P, V, PACK], BF16, name="q0_bf", align_bytes=64)
         q1a_bf = keep.tile([P, HALF, PACK], BF16, name="q1a_bf", tag="stage_c", align_bytes=64)
-        q1b_bf = keep.tile([P, HALF, PACK], BF16, name="q1b_bf", align_bytes=64)
+        q1b_bf = keep.tile([P, HALF, PACK], BF16, name="q1b_bf", tag="stage_d", align_bytes=64)
         interleave(scalar_cast, q0_bf[:], q0_raw[:])
         interleave(scalar_cast, q1a_bf[:], q1a_raw[:])
         q0_codes, q0_scales = quantize(q0_bf, V, "q0")
         q1a = quantize(q1a_bf, HALF, "q1a")
 
         q1b_raw = keep.tile([P, PACK, HALF], F32, name="q1b_raw", tag="stage_a")
-        term_raw = keep.tile([P, PACK, R], F32, name="term_raw", tag="stage_b")
+        term_raw = keep.tile([P, PACK, R], F32, name="term_raw", tag="stage_b", align_bytes=64)
         orig_sb = keep.tile([P, V], F32, name="orig_sb", tag="stage_c", align_bytes=64)
         nc.sync.dma_start(out=q1b_raw[:], in_=q_rows[1][:, :, HALF:V])
         nc.sync.dma_start(out=term_raw[:], in_=term.rearrange("(p j) r -> p j r", j=PACK))
@@ -127,7 +130,7 @@ def tile_picked_yrm3_mix_p_kernel(
                 stop=(g == PASSES - 1),
             )
 
-        banks = [[psum.tile([P, HALF], F32, name="bank%d%d" % (h, j), tag="bank") for j in range(PACK)] for h in range(2)]
+        banks = [[psum.tile([P, HALF], F32, name="bank%d%d" % (h, j), tag="bank%d%d" % (h, j)) for j in range(PACK)] for h in range(2)]
         for h in range(2):
             cols = slice(h * HALF, (h + 1) * HALF)
             for j in range(PACK):
@@ -135,14 +138,14 @@ def tile_picked_yrm3_mix_p_kernel(
 
         picked_words.append(gather_words(1))
         interleave(scalar_cast, q1b_bf[:], q1b_raw[:])
-        q1b = quantize(q1b_bf, HALF, "q1b")
-        term_bf = keep.tile([P, R, PACK], BF16, name="term_bf", align_bytes=64)
-        interleave(nc.vector.tensor_copy, term_bf[:], term_raw[:])
+        q1b = quantize(q1b_bf, HALF, "q1b", tag="word_table1")
+        term_bf = keep.tile([P, R, PACK], BF16, name="term_bf", tag="stage_d", align_bytes=64)
+        interleave(vector_half, term_bf[:], term_raw[:])
         term_codes, term_scales = quantize(term_bf, R, "term")
 
         pd = []
         for h, (codes, scales) in enumerate([q1a, q1b]):
-            pd_h = keep.tile([P, PACK, HALF], F32, name="pd%d" % h)
+            pd_h = keep.tile([P, PACK, HALF], F32, name="pd%d" % h, tag=["stage_a", "pd1"][h])
             for j in range(PACK):
                 score_pass(banks[h][j], 1, j, codes[:], scales[:])
                 nc.scalar.activation(
@@ -150,13 +153,11 @@ def tile_picked_yrm3_mix_p_kernel(
                 )
             pd.append(pd_h)
 
-        half_orig = keep.tile([P, V], F32, name="half_orig")
-        nc.scalar.mul(out=half_orig[:], in_=orig_sb[:], mul=0.5)
 
         lenw_wide = lenw_sb[:].unsqueeze(1).unsqueeze(3).to_broadcast([P, HALF // RUN, PACK, RUN])
         for h in range(2):
             cols = slice(h * HALF, (h + 1) * HALF)
-            wd_bf = keep.tile([P, HALF, PACK], BF16, name="wd_bf%d" % h, align_bytes=64)
+            wd_bf = keep.tile([P, HALF, PACK], BF16, name="wd_bf%d" % h, tag=["stage_b", "stage_d"][h], align_bytes=64)
             nc.vector.tensor_tensor(
                 out=wd_bf[:].rearrange("p (c i) j -> p c j i", i=RUN),
                 in0=pd[h][:].rearrange("p j (c i) -> p c j i", i=RUN),
@@ -164,7 +165,7 @@ def tile_picked_yrm3_mix_p_kernel(
                 op=ALU.mult,
             )
             wd_codes, wd_scales = quantize(wd_bf, HALF, "wd%d" % h)
-            fb = psum.tile([P, HALF], F32, name="fb%d" % h, tag="bank")
+            fb = psum.tile([P, HALF], F32, name="fb%d" % h, tag="bank1%d" % h)
             nc.tensor.matmul_mx(
                 out=fb[:],
                 lhsT=term_codes[:].bitcast(FP8X4),
@@ -176,6 +177,6 @@ def tile_picked_yrm3_mix_p_kernel(
             )
             mixed = keep.tile([P, HALF], F32, name="mixed%d" % h)
             nc.vector.scalar_tensor_tensor(
-                out=mixed[:], in0=fb[:], scalar=0.5, in1=half_orig[:, cols], op0=ALU.mult, op1=ALU.add
+                out=mixed[:], in0=orig_sb[:, cols], scalar=0.5, in1=fb[:], op0=ALU.mult, op1=ALU.add
             )
             nc.sync.dma_start(out=out[:, cols], in_=mixed[:])

@@ -37,24 +37,18 @@ def tile_picked_yrm3_mix_p_kernel(
         keep = ctx.enter_context(tc.tile_pool(name="keep", bufs=1))
         psum = ctx.enter_context(tc.psum_pool(name="psum", bufs=1))
 
-        def quantize(grouped, width, name, tag=None):
-            codes = keep.tile([P, width], U32, name=name + "_codes", tag=tag or name + "_codes", align_bytes=64)
-            scales = keep.tile([P, width], U8, name=name + "_scales", align_bytes=64)
+        def sbuf(shape, dtype, name, slot=None):
+            return keep.tile(shape, dtype, name=name, tag=slot or name, align_bytes=64)
+
+        def quantize(grouped, width, name, slot=None):
+            codes = sbuf([P, width], U32, name + "_codes", slot)
+            scales = sbuf([P, width], U8, name + "_scales")
             nc.vector.quantize_mx(
                 out=codes[:].bitcast(FP8X4),
                 scales=scales[:],
-                in_=grouped[:].rearrange("p w j -> p (w j)"),
+                in_=grouped.rearrange("p w j -> p (w j)"),
             )
             return codes, scales
-
-        scale_table = keep.tile([P, T], U8, name="scale_table", align_bytes=64)
-        nc.vector.memset(scale_table[:].bitcast(I32), 0)
-        scale_queues = [nc.scalar, nc.scalar, nc.scalar, nc.scalar]
-        for quad in range(4):
-            scale_queues[quad].dma_start(
-                out=scale_table[32 * quad : 32 * quad + 4 * PASSES, :].bitcast(I32),
-                in_=x_scales[:, 4 * quad : 4 * quad + 4, :].bitcast(I32),
-            )
 
         def vector_half(out, in_):
             nc.vector.tensor_scalar(out=out, in0=in_, scalar1=0.5, scalar2=None, op0=ALU.mult)
@@ -62,15 +56,17 @@ def tile_picked_yrm3_mix_p_kernel(
         def scalar_cast(out, in_):
             nc.scalar.activation(out=out, in_=in_, func=ACT.Copy)
 
-        prior_sb = keep.tile([P, PACK], F32, name="prior_sb")
-        lenw_sb = keep.tile([P, PACK], F32, name="lenw_sb")
-        nc.gpsimd.dma_start(out=prior_sb[:], in_=prior.rearrange("(p j) o -> p (j o)", j=PACK))
-        nc.gpsimd.dma_start(out=lenw_sb[:], in_=lenw.rearrange("(p j) o -> p (j o)", j=PACK))
+        scale_table = sbuf([P, T], U8, "scale_table")
+        nc.gpsimd.memset(scale_table[:].bitcast(I32), 0)
+        for quad in range(4):
+            nc.gpsimd.dma_start(
+                out=scale_table[32 * quad : 32 * quad + 4 * PASSES, :].bitcast(I32),
+                in_=x_scales[:, 4 * quad : 4 * quad + 4, :].bitcast(I32),
+            )
 
         offsets = keep.tile([P, S // 16], U16, name="offsets")
-        nc.sync.dma_start(offsets[:], offs)
 
-        word_table = [keep.tile([P, T], U32, name="word_table%d" % g, tag="word_table%d" % g, align_bytes=64) for g in range(PASSES)]
+        word_table = [sbuf([P, T], U32, "word_table%d" % g) for g in range(PASSES)]
 
         def load_words(g):
             nc.sync.dma_start(
@@ -79,15 +75,26 @@ def tile_picked_yrm3_mix_p_kernel(
             )
 
         q_rows = qT.rearrange("(g p j) v -> g p j v", g=PASSES, j=PACK)
-        q0_raw = keep.tile([P, PACK, V], F32, name="q0_raw", tag="stage_a")
-        q1a_raw = keep.tile([P, PACK, HALF], F32, name="q1a_raw", tag="stage_b", align_bytes=64)
+        q0_raw = sbuf([P, PACK, V], F32, "q0_raw")
+        q1a_raw = sbuf([P, PACK, HALF], F32, "q1a_raw")
+        q1b_raw = sbuf([P, PACK, HALF], F32, "q1b_raw")
+        prior_sb = sbuf([P, PACK], F32, "prior_sb")
+        lenw_sb = sbuf([P, PACK], F32, "lenw_sb")
+        term_raw = sbuf([P, PACK, R], F32, "term_raw")
+        orig_sb = sbuf([P, V], F32, "orig_sb")
         load_words(0)
+        nc.sync.dma_start(offsets[:], offs)
         nc.sync.dma_start(out=q0_raw[:], in_=q_rows[0])
         nc.sync.dma_start(out=q1a_raw[:], in_=q_rows[1][:, :, 0:HALF])
         load_words(1)
+        nc.sync.dma_start(out=q1b_raw[:], in_=q_rows[1][:, :, HALF:V])
+        nc.sync.dma_start(out=prior_sb[:], in_=prior.rearrange("(p j) o -> p (j o)", j=PACK))
+        nc.sync.dma_start(out=lenw_sb[:], in_=lenw.rearrange("(p j) o -> p (j o)", j=PACK))
+        nc.sync.dma_start(out=term_raw[:], in_=term.rearrange("(p j) r -> p j r", j=PACK))
+        nc.sync.dma_start(out=orig_sb[:], in_=orig)
 
-        def gather_words(g):
-            picked = keep.tile([P, S], U32, name="picked_words%d" % g, align_bytes=64)
+        def gather_words(g, slot=None):
+            picked = sbuf([P, S], U32, "picked_words%d" % g, slot)
             nc.vector.tensor_copy(
                 out=picked[:].rearrange("p (j m) -> p m j", j=PACK),
                 in_=word_table[g][:].indirect(offsets[:]),
@@ -95,28 +102,20 @@ def tile_picked_yrm3_mix_p_kernel(
             return picked
 
         picked_words = [gather_words(0)]
-        listed_scales = keep.tile([P, S], U8, name="listed_scales", align_bytes=64)
-        picked_scales = keep.tile([P, S], U8, name="picked_scales", align_bytes=64)
+        listed_scales = sbuf([P, S], U8, "listed_scales", "word_table0")
+        picked_scales = sbuf([P, S], U8, "picked_scales")
         nc.vector.tensor_copy(out=listed_scales[:], in_=scale_table[:].indirect(offsets[:]))
         nc.vector.tensor_copy(
             out=picked_scales[:].rearrange("p (j m) -> p j m", j=PACK),
             in_=listed_scales[:].rearrange("p (m j) -> p j m", j=PACK),
         )
 
-        q0_bf = keep.tile([P, V, PACK], BF16, name="q0_bf", align_bytes=64)
-        q1a_bf = keep.tile([P, HALF, PACK], BF16, name="q1a_bf", tag="stage_c", align_bytes=64)
-        q1b_bf = keep.tile([P, HALF, PACK], BF16, name="q1b_bf", tag="stage_d", align_bytes=64)
+        q0_bf = sbuf([P, V, PACK], BF16, "q0_bf")
+        q1a_bf = sbuf([P, HALF, PACK], BF16, "q1a_bf")
         interleave(scalar_cast, q0_bf[:], q0_raw[:])
         interleave(scalar_cast, q1a_bf[:], q1a_raw[:])
-        q0_codes, q0_scales = quantize(q0_bf, V, "q0")
-        q1a = quantize(q1a_bf, HALF, "q1a")
-
-        q1b_raw = keep.tile([P, PACK, HALF], F32, name="q1b_raw", tag="stage_a")
-        term_raw = keep.tile([P, PACK, R], F32, name="term_raw", tag="stage_b", align_bytes=64)
-        orig_sb = keep.tile([P, V], F32, name="orig_sb", tag="stage_c", align_bytes=64)
-        nc.sync.dma_start(out=q1b_raw[:], in_=q_rows[1][:, :, HALF:V])
-        nc.sync.dma_start(out=term_raw[:], in_=term.rearrange("(p j) r -> p j r", j=PACK))
-        nc.sync.dma_start(out=orig_sb[:], in_=orig)
+        q0_codes, q0_scales = quantize(q0_bf[:], V, "q0", "scale_table")
+        q1a = quantize(q1a_bf[:], HALF, "q1a")
 
         def score_pass(bank, g, j, codes, scales):
             cols = slice(j * P, (j + 1) * P)
@@ -130,41 +129,44 @@ def tile_picked_yrm3_mix_p_kernel(
                 stop=(g == PASSES - 1),
             )
 
-        banks = [[psum.tile([P, HALF], F32, name="bank%d%d" % (h, j), tag="bank%d%d" % (h, j)) for j in range(PACK)] for h in range(2)]
+        banks = [
+            [psum.tile([P, HALF], F32, name="bank%d%d" % (h, j), tag="bank%d%d" % (h, j)) for j in range(PACK)]
+            for h in range(2)
+        ]
         for h in range(2):
             cols = slice(h * HALF, (h + 1) * HALF)
             for j in range(PACK):
                 score_pass(banks[h][j], 0, j, q0_codes[:, cols], q0_scales[:, cols])
 
-        picked_words.append(gather_words(1))
+        picked_words.append(gather_words(1, "word_table0"))
+        q1b_bf = sbuf([P, HALF, PACK], BF16, "q1b_bf")
         interleave(scalar_cast, q1b_bf[:], q1b_raw[:])
-        q1b = quantize(q1b_bf, HALF, "q1b", tag="word_table1")
-        term_bf = keep.tile([P, R, PACK], BF16, name="term_bf", tag="stage_d", align_bytes=64)
+        q1b = quantize(q1b_bf[:], HALF, "q1b", "word_table1")
+        term_bf = sbuf([P, R, PACK], BF16, "term_bf", "q1b_bf")
         interleave(vector_half, term_bf[:], term_raw[:])
-        term_codes, term_scales = quantize(term_bf, R, "term")
+        term_codes, term_scales = quantize(term_bf[:], R, "term")
 
-        pd = []
+        lenw_wide = lenw_sb[:].unsqueeze(1).unsqueeze(3).to_broadcast([P, HALF // RUN, PACK, RUN])
+
+        wd = []
         for h, (codes, scales) in enumerate([q1a, q1b]):
-            pd_h = keep.tile([P, PACK, HALF], F32, name="pd%d" % h, tag=["stage_a", "pd1"][h])
+            pd = sbuf([P, PACK, HALF], F32, "pd%d" % h, ["q1b_raw", None][h])
             for j in range(PACK):
                 score_pass(banks[h][j], 1, j, codes[:], scales[:])
                 nc.scalar.activation(
-                    out=pd_h[:, j, :], in_=banks[h][j][:], func=ACT.Exp, bias=prior_sb[:, j : j + 1], scale=0.8
+                    out=pd[:, j, :], in_=banks[h][j][:], func=ACT.Exp, bias=prior_sb[:, j : j + 1], scale=0.8
                 )
-            pd.append(pd_h)
-
-
-        lenw_wide = lenw_sb[:].unsqueeze(1).unsqueeze(3).to_broadcast([P, HALF // RUN, PACK, RUN])
-        for h in range(2):
-            cols = slice(h * HALF, (h + 1) * HALF)
-            wd_bf = keep.tile([P, HALF, PACK], BF16, name="wd_bf%d" % h, tag=["stage_b", "stage_d"][h], align_bytes=64)
+            wd_bf = sbuf([P, HALF, PACK], BF16, "wd_bf%d" % h, ["term_raw", None][h])
             nc.vector.tensor_tensor(
                 out=wd_bf[:].rearrange("p (c i) j -> p c j i", i=RUN),
-                in0=pd[h][:].rearrange("p j (c i) -> p c j i", i=RUN),
+                in0=pd[:].rearrange("p j (c i) -> p c j i", i=RUN),
                 in1=lenw_wide,
                 op=ALU.mult,
             )
-            wd_codes, wd_scales = quantize(wd_bf, HALF, "wd%d" % h)
+            wd.append(quantize(wd_bf[:], HALF, "wd%d" % h))
+
+        for h, (wd_codes, wd_scales) in enumerate(wd):
+            cols = slice(h * HALF, (h + 1) * HALF)
             fb = psum.tile([P, HALF], F32, name="fb%d" % h, tag="bank1%d" % h)
             nc.tensor.matmul_mx(
                 out=fb[:],
@@ -175,7 +177,7 @@ def tile_picked_yrm3_mix_p_kernel(
                 start=True,
                 stop=True,
             )
-            mixed = keep.tile([P, HALF], F32, name="mixed%d" % h)
+            mixed = sbuf([P, HALF], F32, "mixed%d" % h)
             nc.vector.scalar_tensor_tensor(
                 out=mixed[:], in0=orig_sb[:, cols], scalar=0.5, in1=fb[:], op0=ALU.mult, op1=ALU.add
             )

@@ -57,12 +57,7 @@ def tile_picked_yrm3_mix_p_kernel(
             nc.scalar.activation(out=out, in_=in_, func=ACT.Copy)
 
         scale_table = sbuf([P, T], U8, "scale_table")
-        nc.gpsimd.memset(scale_table[:].bitcast(I32), 0)
-        for quad in range(4):
-            nc.gpsimd.dma_start(
-                out=scale_table[32 * quad : 32 * quad + 4 * PASSES, :].bitcast(I32),
-                in_=x_scales[:, 4 * quad : 4 * quad + 4, :].bitcast(I32),
-            )
+        nc.vector.memset(scale_table[:].bitcast(I32), 0)
 
         offsets = keep.tile([P, S // 16], U16, name="offsets")
 
@@ -82,14 +77,19 @@ def tile_picked_yrm3_mix_p_kernel(
         lenw_sb = sbuf([P, PACK], F32, "lenw_sb")
         term_raw = sbuf([P, PACK, R], F32, "term_raw")
         orig_sb = sbuf([P, V], F32, "orig_sb")
-        load_words(0)
         nc.sync.dma_start(offsets[:], offs)
+        load_words(0)
+        for quad in range(4):
+            nc.sync.dma_start(
+                out=scale_table[32 * quad : 32 * quad + 4 * PASSES, :].bitcast(I32),
+                in_=x_scales[:, 4 * quad : 4 * quad + 4, :].bitcast(I32),
+            )
         nc.sync.dma_start(out=q0_raw[:], in_=q_rows[0])
         nc.sync.dma_start(out=q1a_raw[:], in_=q_rows[1][:, :, 0:HALF])
         load_words(1)
         nc.sync.dma_start(out=q1b_raw[:], in_=q_rows[1][:, :, HALF:V])
-        nc.sync.dma_start(out=prior_sb[:], in_=prior.rearrange("(p j) o -> p (j o)", j=PACK))
-        nc.sync.dma_start(out=lenw_sb[:], in_=lenw.rearrange("(p j) o -> p (j o)", j=PACK))
+        nc.gpsimd.dma_start(out=prior_sb[:], in_=prior.rearrange("(p j) o -> p (j o)", j=PACK))
+        nc.gpsimd.dma_start(out=lenw_sb[:], in_=lenw.rearrange("(p j) o -> p (j o)", j=PACK))
         nc.sync.dma_start(out=term_raw[:], in_=term.rearrange("(p j) r -> p j r", j=PACK))
         nc.sync.dma_start(out=orig_sb[:], in_=orig)
 
@@ -102,7 +102,7 @@ def tile_picked_yrm3_mix_p_kernel(
             return picked
 
         picked_words = [gather_words(0)]
-        listed_scales = sbuf([P, S], U8, "listed_scales", "word_table0")
+        listed_scales = sbuf([P, S], U8, "listed_scales")
         picked_scales = sbuf([P, S], U8, "picked_scales")
         nc.vector.tensor_copy(out=listed_scales[:], in_=scale_table[:].indirect(offsets[:]))
         nc.vector.tensor_copy(
@@ -114,7 +114,7 @@ def tile_picked_yrm3_mix_p_kernel(
         q1a_bf = sbuf([P, HALF, PACK], BF16, "q1a_bf")
         interleave(scalar_cast, q0_bf[:], q0_raw[:])
         interleave(scalar_cast, q1a_bf[:], q1a_raw[:])
-        q0_codes, q0_scales = quantize(q0_bf[:], V, "q0", "scale_table")
+        q0_codes, q0_scales = quantize(q0_bf[:], V, "q0")
         q1a = quantize(q1a_bf[:], HALF, "q1a")
 
         def score_pass(bank, g, j, codes, scales):
@@ -138,7 +138,7 @@ def tile_picked_yrm3_mix_p_kernel(
             for j in range(PACK):
                 score_pass(banks[h][j], 0, j, q0_codes[:, cols], q0_scales[:, cols])
 
-        picked_words.append(gather_words(1, "word_table0"))
+        picked_words.append(gather_words(1))
         q1b_bf = sbuf([P, HALF, PACK], BF16, "q1b_bf")
         interleave(scalar_cast, q1b_bf[:], q1b_raw[:])
         q1b = quantize(q1b_bf[:], HALF, "q1b", "word_table1")

from contextlib import ExitStack

import concourse.mybir as mybir

K, T, S, V, R = 1024, 2048, 512, 256, 128
FLOPS = 2 * K * S * V + 2 * S * R * V

F32 = mybir.dt.float32
BF16 = mybir.dt.bfloat16
I32 = mybir.dt.int32
U32 = mybir.dt.uint32
U16 = mybir.dt.uint16
U8 = mybir.dt.uint8
FP8X4 = mybir.dt.float8_e4m3fn_x4
ACT = mybir.ActivationFunctionType
ALU = mybir.AluOpType

P = 128
PACK = 4
PASSES = K // (P * PACK)
HALF = V // 2
RUN = 4


def interleave(copy, grouped, raw):
    copy(
        out=grouped.rearrange("p (c i) j -> p c j i", i=RUN),
        in_=raw.rearrange("p j (c i) -> p c j i", i=RUN),
    )


def tile_picked_yrm3_mix_p_kernel(
    tc, x_words, x_scales, qT, term, prior, lenw, orig, offs, out
):
    nc = tc.nc
    with ExitStack() as ctx:
        keep = ctx.enter_context(tc.tile_pool(name="keep", bufs=1))
        psum = ctx.enter_context(tc.psum_pool(name="psum", bufs=1))

        def sbuf(shape, dtype, name, slot=None):
            return keep.tile(shape, dtype, name=name, tag=slot or name, align_bytes=64)

        def quantize(grouped, width, name, slot=None):
            codes = sbuf([P, width], U32, name + "_codes", slot)
            scales = sbuf([P, width], U8, name + "_scales")
            nc.vector.quantize_mx(
                out=codes[:].bitcast(FP8X4),
                scales=scales[:],
                in_=grouped.rearrange("p w j -> p (w j)"),
            )
            return codes, scales

        def vector_half(out, in_):
            nc.vector.tensor_scalar(out=out, in0=in_, scalar1=0.5, scalar2=None, op0=ALU.mult)

        def scalar_cast(out, in_):
            nc.scalar.activation(out=out, in_=in_, func=ACT.Copy)

        scale_table = sbuf([P, T], U8, "scale_table")
        nc.vector.memset(scale_table[:].bitcast(I32), 0)

        offsets = keep.tile([P, S // 16], U16, name="offsets")

        word_table = [sbuf([P, T], U32, "word_table%d" % g) for g in range(PASSES)]

        def load_words(g):
            nc.sync.dma_start(
                out=word_table[g][:].bitcast(I32),
                in_=x_words[g].rearrange("p n t -> p (n t)").bitcast(I32),
            )

        q_rows = qT.rearrange("(g p j) v -> g p j v", g=PASSES, j=PACK)
        q0_raw = sbuf([P, PACK, V], F32, "q0_raw")
        q1a_raw = sbuf([P, PACK, HALF], F32, "q1a_raw")
        q1b_raw = sbuf([P, PACK, HALF], F32, "q1b_raw")
        prior_sb = sbuf([P, PACK], F32, "prior_sb")
        lenw_sb = sbuf([P, PACK], F32, "lenw_sb")
        term_raw = sbuf([P, PACK, R], F32, "term_raw")
        orig_sb = sbuf([P, V], F32, "orig_sb")
        nc.sync.dma_start(offsets[:], offs)
        load_words(0)
        for quad in range(4):
            nc.sync.dma_start(
                out=scale_table[32 * quad : 32 * quad + 4 * PASSES, :].bitcast(I32),
                in_=x_scales[:, 4 * quad : 4 * quad + 4, :].bitcast(I32),
            )
        nc.sync.dma_start(out=q0_raw[:], in_=q_rows[0])
        nc.sync.dma_start(out=q1a_raw[:], in_=q_rows[1][:, :, 0:HALF])
        load_words(1)
        nc.sync.dma_start(out=q1b_raw[:], in_=q_rows[1][:, :, HALF:V])
        nc.gpsimd.dma_start(out=prior_sb[:], in_=prior.rearrange("(p j) o -> p (j o)", j=PACK))
        nc.gpsimd.dma_start(out=lenw_sb[:], in_=lenw.rearrange("(p j) o -> p (j o)", j=PACK))
        nc.sync.dma_start(out=term_raw[:], in_=term.rearrange("(p j) r -> p j r", j=PACK))
        nc.sync.dma_start(out=orig_sb[:], in_=orig)

        def gather_words(g, slot=None):
            picked = sbuf([P, S], U32, "picked_words%d" % g, slot)
            nc.vector.tensor_copy(
                out=picked[:].rearrange("p (j m) -> p m j", j=PACK),
                in_=word_table[g][:].indirect(offsets[:]),
            )
            return picked

        picked_words = [gather_words(0)]
        listed_scales = sbuf([P, S], U8, "listed_scales")
        picked_scales = sbuf([P, S], U8, "picked_scales")
        nc.vector.tensor_copy(out=listed_scales[:], in_=scale_table[:].indirect(offsets[:]))
        nc.vector.tensor_copy(
            out=picked_scales[:].rearrange("p (j m) -> p j m", j=PACK),
            in_=listed_scales[:].rearrange("p (m j) -> p j m", j=PACK),
        )

        q0_bf = sbuf([P, V, PACK], BF16, "q0_bf")
        q1a_bf = sbuf([P, HALF, PACK], BF16, "q1a_bf")
        interleave(scalar_cast, q0_bf[:], q0_raw[:])
        interleave(scalar_cast, q1a_bf[:], q1a_raw[:])
        q0_codes, q0_scales = quantize(q0_bf[:], V, "q0")
        q1a = quantize(q1a_bf[:], HALF, "q1a")

        def score_pass(bank, g, j, codes, scales):
            cols = slice(j * P, (j + 1) * P)
            nc.tensor.matmul_mx(
                out=bank[:],
                lhsT=picked_words[g][:, cols].bitcast(FP8X4),
                lhsT_scale=picked_scales[4 * g :, cols],
                rhs=codes.bitcast(FP8X4),
                rhs_scale=scales,
                start=(g == 0),
                stop=(g == PASSES - 1),
            )

        banks = [
            [psum.tile([P, HALF], F32, name="bank%d%d" % (h, j), tag="bank%d%d" % (h, j)) for j in range(PACK)]
            for h in range(2)
        ]
        for h in range(2):
            cols = slice(h * HALF, (h + 1) * HALF)
            for j in range(PACK):
                score_pass(banks[h][j], 0, j, q0_codes[:, cols], q0_scales[:, cols])

        picked_words.append(gather_words(1))
        q1b_bf = sbuf([P, HALF, PACK], BF16, "q1b_bf")
        interleave(scalar_cast, q1b_bf[:], q1b_raw[:])
        q1b = quantize(q1b_bf[:], HALF, "q1b", "word_table1")
        term_bf = sbuf([P, R, PACK], BF16, "term_bf", "q1b_bf")
        interleave(vector_half, term_bf[:], term_raw[:])
        term_codes, term_scales = quantize(term_bf[:], R, "term")

        lenw_wide = lenw_sb[:].unsqueeze(1).unsqueeze(3).to_broadcast([P, HALF // RUN, PACK, RUN])

        wd = []
        for h, (codes, scales) in enumerate([q1a, q1b]):
            pd = sbuf([P, PACK, HALF], F32, "pd%d" % h, ["q1b_raw", None][h])
            for j in range(PACK):
                score_pass(banks[h][j], 1, j, codes[:], scales[:])
                nc.scalar.activation(
                    out=pd[:, j, :], in_=banks[h][j][:], func=ACT.Exp, bias=prior_sb[:, j : j + 1], scale=0.8
                )
            wd_bf = sbuf([P, HALF, PACK], BF16, "wd_bf%d" % h, ["term_raw", None][h])
            nc.vector.tensor_tensor(
                out=wd_bf[:].rearrange("p (c i) j -> p c j i", i=RUN),
                in0=pd[:].rearrange("p j (c i) -> p c j i", i=RUN),
                in1=lenw_wide,
                op=ALU.mult,
            )
            wd.append(quantize(wd_bf[:], HALF, "wd%d" % h))

        for h, (wd_codes, wd_scales) in enumerate(wd):
            cols = slice(h * HALF, (h + 1) * HALF)
            fb = psum.tile([P, HALF], F32, name="fb%d" % h, tag="bank1%d" % h)
            nc.tensor.matmul_mx(
                out=fb[:],
                lhsT=term_codes[:].bitcast(FP8X4),
                lhsT_scale=term_scales[:],
                rhs=wd_codes[:].bitcast(FP8X4),
                rhs_scale=wd_scales[:],
                start=True,
                stop=True,
            )
            mixed = sbuf([P, HALF], F32, "mixed%d" % h)
            nc.vector.scalar_tensor_tensor(
                out=mixed[:], in0=orig_sb[:, cols], scalar=0.5, in1=fb[:], op0=ALU.mult, op1=ALU.add
            )
            nc.sync.dma_start(out=out[:, cols], in_=mixed[:])
